import numpy as np
import ml_dtypes


def mxq(x, axis, fmt="e4m3"):
    dtype, down = {"e4m3": (ml_dtypes.float8_e4m3fn, 7), "e5m2": (ml_dtypes.float8_e5m2, 14)}[fmt]
    v = np.moveaxis(np.asarray(x, np.float32).astype(ml_dtypes.bfloat16).astype(np.float64), axis, -1)
    blocks = v.reshape(v.shape[:-1] + (-1, 32))
    amax = np.abs(blocks).max(-1, keepdims=True)
    byte = np.maximum(np.where(amax > 0, np.frexp(amax)[1] - 1 + 127, 0) - down, 1)
    scale = np.exp2(byte - 127.0)
    codes = (blocks / scale).astype(np.float32).astype(dtype).astype(np.float64)
    return np.moveaxis((codes * scale).reshape(v.shape), -1, axis)


WIDE = False


def mx_kscale(k):
    if not WIDE:
        return np.ones(k)
    levels = np.array([10, -10, 5, -5, 0])
    if k % 512:
        return np.exp2(np.random.permutation(np.resize(levels, k // 32))).repeat(32)
    a = np.empty((k // 512, 16))
    for p in range(k // 512):
        a[p, :8] = np.random.permutation(np.resize(levels, 8))
        for g in range(8):
            far = levels[np.abs(levels - a[p, g]) >= 10]
            a[p, g + 8] = far[np.random.randint(len(far))]
    return np.exp2(a.ravel()).repeat(32)


def f64(x):
    return np.asarray(x).astype(np.float64)


def striped(idx):
    return np.tile(np.asarray(idx).reshape(-1, 16).T, (8, 1)).astype(np.uint16)


def unstriped(offs):
    return offs[:16].T.reshape(-1).astype(np.int64)


E2M1 = np.array([0.0, 0.5, 1.0, 1.5, 2.0, 3.0, 4.0, 6.0, -0.0, -0.5, -1.0, -1.5, -2.0, -3.0, -4.0, -6.0])


def pack_weight(w, fmt):
    k, n = w.shape
    w = f64(np.asarray(w, np.float32).astype(ml_dtypes.bfloat16)).reshape(k // 32, 32, n)
    amax = np.abs(w).max(1)
    if fmt == "e4m3":
        byte = np.frexp(amax)[1] - 1 + 127 - 7
    else:
        mant, ex = np.frexp(amax / 6.0)
        byte = np.where(mant > 0.5, ex, ex - 1) + 127
    byte = np.clip(np.where(amax > 0, byte, 1), 1, 254)
    scaled = (w * np.exp2(127.0 - byte)[:, None, :]).reshape(k, n).astype(np.float32)
    by_word = np.ascontiguousarray(scaled.reshape(k // 512, 128, 4, n).transpose(0, 1, 3, 2))
    if fmt == "e4m3":
        words = by_word.astype(ml_dtypes.float8_e4m3fn).view(np.uint8)
    else:
        c = by_word.astype(ml_dtypes.float4_e2m1fn).view(np.uint8) & 0xF
        words = (c[..., 0::2] | (c[..., 1::2] << 4)).reshape(k // 512, 128, 2 * n)
    return np.ascontiguousarray(words), np.ascontiguousarray(byte.astype(np.uint8).reshape(k // 512, 16, n))


def unpack_weight(words, scales, fmt):
    g, _, n = scales.shape
    words = np.ascontiguousarray(words).reshape(g, 128, n, -1)
    if fmt == "e4m3":
        vals = words.view(ml_dtypes.float8_e4m3fn).astype(np.float64)
    else:
        nib = np.empty((g, 128, n, 4), np.uint8)
        nib[..., 0::2] = words & 0xF
        nib[..., 1::2] = words >> 4
        vals = E2M1[nib]
    vals = vals * np.repeat(np.exp2(scales.astype(np.float64) - 127.0), 8, axis=1)[..., None]
    return vals.transpose(0, 1, 3, 2).reshape(g * 512, n)


K, T, J, N = 1024, 2048, 512, 512


def setup_inputs():
    n = np.random.standard_normal
    idx = np.random.permutation(T)[:J]
    idx2 = np.random.permutation(T)[:J]
    fk = mx_kscale(K)
    xtp = pack_weight(n((K, T)) * np.random.uniform(0.3, 1.7, (1, T)) / fk[:, None], "e4m3")
    wbp = pack_weight(n((K, N)) * 1 / np.sqrt(K) * fk[:, None], "e2m1")
    return {
        "xt_words": xtp[0],
        "xt_scales": xtp[1],
        "wa": (n((K, N)) * 1 / np.sqrt(K) * fk[:, None]).astype(np.float32),
        "wb_words": wbp[0],
        "wb_scales": wbp[1],
        "offs": striped(idx),
        "offs2": striped(idx2),
    }


def reference(xt_words, xt_scales, wa, wb_words, wb_scales, offs, offs2):
    idx = unstriped(offs)
    idx2 = unstriped(offs2)
    xtu = unpack_weight(xt_words, xt_scales, "e4m3")
    wbu = unpack_weight(wb_words, wb_scales, "e2m1")
    xtidxg = xtu[:, idx]
    waq = mxq(f64(wa), 0, "e4m3")
    a = xtidxg.T @ waq
    xtidx2g = xtu[:, idx2]
    b = xtidx2g.T @ wbu
    sa = np.sqrt(np.mean(np.square(a), axis=1, keepdims=True) + 0.01)
    sb = np.sqrt(np.mean(np.square(b), axis=1, keepdims=True) + 0.01)
    y = a * sb / sa + 0.3 * b
    return y

@@ -1,0 +1,158 @@
+from contextlib import ExitStack
+
+import concourse.mybir as mybir
+
+K, T, J, N = 1024, 2048, 512, 512
+FLOPS = 2 * 2 * J * N * K
+
+F32 = mybir.dt.float32
+BF16 = mybir.dt.bfloat16
+I32 = mybir.dt.int32
+U32 = mybir.dt.uint32
+U16 = mybir.dt.uint16
+U8 = mybir.dt.uint8
+FP8X4 = mybir.dt.float8_e4m3fn_x4
+FP4X4 = mybir.dt.float4_e2m1fn_x4
+ACT = mybir.ActivationFunctionType
+MULT = mybir.AluOpType.mult
+ADD = mybir.AluOpType.add
+
+P = 128
+PASSES = 2
+BLOCKS = J // P
+HALF = N // 2
+EPS_SUM = 0.01 * N
+
+
+def tile_moe_expert_sized_like_other_kernel(tc, xt_words, xt_scales, wa, wb_words, wb_scales, offs, offs2, out):
+    nc = tc.nc
+    with ExitStack() as ctx:
+        sb = ctx.enter_context(tc.tile_pool(name="sb", bufs=1))
+        psum = ctx.enter_context(tc.psum_pool(name="psum", bufs=1))
+
+        list_a = sb.tile([P, J // 16], U16, name="list_a")
+        list_b = sb.tile([P, J // 16], U16, name="list_b")
+        x_words = [sb.tile([P, T], I32, name="x_words%d" % z, align_bytes=64) for z in range(PASSES)]
+        x_scales = sb.tile([P, T], U8, name="x_scales", align_bytes=64)
+        wb_codes = sb.tile([P, PASSES, 2 * N], U8, name="wb_codes", align_bytes=64)
+        wb_plane = sb.tile([P, PASSES, N], U8, name="wb_plane", align_bytes=64)
+        xb_plane1 = sb.tile([P, J], U8, name="xb_plane1", align_bytes=64)
+        zero = sb.tile([P, 1], F32, name="zero")
+
+        nc.vector.memset(x_scales[:].bitcast(I32), 0)
+        nc.vector.memset(wb_plane[:].rearrange("p z c -> p (z c)").bitcast(I32), 0)
+        nc.vector.memset(xb_plane1[:].bitcast(I32), 0)
+        nc.vector.memset(zero[:], 0.0)
+
+        nc.sync.dma_start(list_b[:], offs2)
+        nc.sync.dma_start(list_a[:], offs)
+        nc.sync.dma_start(wb_codes[:].bitcast(I32), wb_words.rearrange("z p c -> p z c").bitcast(I32))
+        for q in range(4):
+            nc.sync.dma_start(x_scales[32 * q : 32 * q + 8, :].bitcast(I32), xt_scales[:, 4 * q : 4 * q + 4, :].bitcast(I32))
+        nc.sync.dma_start(x_words[0][:], xt_words[0].rearrange("p c t -> p (c t)").bitcast(I32))
+        for r in range(4):
+            nc.sync.dma_start(wb_plane[r:P:32, :, :].bitcast(I32), wb_scales.rearrange("z (q r) c -> r q z c", r=4)[r].bitcast(I32))
+        nc.sync.dma_start(x_words[1][:], xt_words[1].rearrange("p c t -> p (c t)").bitcast(I32))
+        wa_raw = {}
+        for h in range(2):
+            for z in range(PASSES):
+                wa_raw[h, z] = sb.tile([P, 4, HALF], F32, name="wa_raw%d_%d" % (h, z))
+                nc.sync.dma_start(wa_raw[h, z][:], wa[512 * z : 512 * (z + 1), h * HALF : (h + 1) * HALF].rearrange("(p t) c -> p t c", t=4))
+
+        root_eps = sb.tile([P, 1], F32, name="root_eps")
+        nc.scalar.activation(root_eps[:], zero[:], ACT.Abs_reciprocal_sqrt, bias=1.0 / EPS_SUM)
+
+        xa_plane = sb.tile([P, J], U8, name="xa_plane", align_bytes=64)
+        xb_plane = sb.tile([P, J], U8, name="xb_plane", align_bytes=64)
+        xa = [sb.tile([P, J], U32, name="xa%d" % z, align_bytes=64) for z in range(PASSES)]
+        xb = [sb.tile([P, J], U32, name="xb%d" % z, align_bytes=64) for z in range(PASSES)]
+        nc.vector.tensor_copy(xb_plane[:], x_scales[:].indirect(list_b[:]))
+        nc.scalar.dma_start(xb_plane1[0:100, :].bitcast(I32), xb_plane[4:104, :].bitcast(I32))
+        nc.vector.tensor_copy(xa_plane[:], x_scales[:].indirect(list_a[:]))
+        nc.vector.tensor_copy(xb[0][:], x_words[0][:].bitcast(U32).indirect(list_b[:]))
+        nc.vector.tensor_copy(xa[0][:], x_words[0][:].bitcast(U32).indirect(list_a[:]))
+        for h in range(2):
+            nc.vector.tensor_copy(xb[1][:, h * 256 : (h + 1) * 256], x_words[1][:].bitcast(U32).indirect(list_b[:, h * 16 : (h + 1) * 16]))
+        nc.vector.tensor_copy(xa[1][:], x_words[1][:].bitcast(U32).indirect(list_a[:]))
+
+
+        b_sums = [psum.tile([P, N], F32, name="b_sums%d" % i, tag="bank_b%d" % i) for i in range(BLOCKS)]
+        xb_planes = [xb_plane, xb_plane1]
+        for z in range(PASSES):
+            for i in range(BLOCKS):
+                slots = slice(i * P, (i + 1) * P)
+                nc.tensor.matmul_mx(
+                    out=b_sums[i][:],
+                    lhsT=xb[z][:, slots].bitcast(FP8X4),
+                    lhsT_scale=xb_planes[z][:, slots],
+                    rhs=wb_codes[:, z, :].bitcast(FP4X4),
+                    rhs_scale=wb_plane[:, z, :],
+                    start=(z == 0),
+                    stop=(z == PASSES - 1),
+                )
+
+        ssq_b = sb.tile([P, BLOCKS], F32, name="ssq_b")
+        inv_b = sb.tile([P, BLOCKS], F32, name="inv_b")
+        eps_a = sb.tile([P, BLOCKS], F32, name="eps_a")
+        squares = sb.tile([P, 2 * BLOCKS, N], BF16, name="squares")
+        for i in range(BLOCKS):
+            nc.scalar.activation(squares[:, i, :], b_sums[i][:], ACT.Square, accum_out=ssq_b[:, i : i + 1])
+        nc.scalar.activation(inv_b[:], ssq_b[:], ACT.Abs_reciprocal_sqrt, bias=EPS_SUM)
+        nc.scalar.activation(eps_a[:], inv_b[:], ACT.Square, scale=root_eps[:])
+
+        codes, planes = {}, {}
+        for h in range(2):
+            for z in range(PASSES):
+                grouped = sb.tile([P, HALF, 4], BF16, name="grouped%d_%d" % (h, z), tag="staging%d" % (0, 1, 2, 1)[2 * h + z], align_bytes=64)
+                codes[h, z] = sb.tile([P, HALF], U32, name="codes%d_%d" % (h, z), align_bytes=64)
+                planes[h, z] = sb.tile([P, HALF], U8, name="plane%d_%d" % (h, z), align_bytes=64)
+                if (h, z) in ((0, 0), (0, 1), (1, 0)):
+                    nc.gpsimd.tensor_scalar(grouped[:], wa_raw[h, z][:].rearrange("p t c -> p c t"), 1.0, 0.0, MULT, ADD)
+                elif (h, z) in ():
+                    nc.scalar.copy(
+                        grouped[:].rearrange("p (c i) t -> p c t i", i=4),
+                        wa_raw[h, z][:].rearrange("p t (c i) -> p c t i", i=4),
+                    )
+                else:
+                    nc.vector.tensor_copy(
+                        grouped[:].rearrange("p (c i) t -> p c t i", i=4),
+                        wa_raw[h, z][:].rearrange("p t (c i) -> p c t i", i=4),
+                    )
+                nc.vector.quantize_mx(out=codes[h, z][:].bitcast(FP8X4), scales=planes[h, z][:], in_=grouped[:].rearrange("p c t -> p (c t)"))
+
+        a_sums = [psum.tile([P, N], F32, name="a_sums%d" % i) for i in range(BLOCKS)]
+        ssq_a = [sb.tile([P, BLOCKS], F32, name="ssq_a%d" % h) for h in range(2)]
+        for h in range(2):
+            cols = slice(h * HALF, (h + 1) * HALF)
+            for z, i in [(z, i) for z in range(PASSES) for i in range(BLOCKS)]:
+                slots = slice(i * P, (i + 1) * P)
+                nc.tensor.matmul_mx(
+                    out=a_sums[i][:, cols],
+                    lhsT=xa[z][:, slots].bitcast(FP8X4),
+                    lhsT_scale=xa_plane[4 * z :, slots],
+                    rhs=codes[h, z][:].bitcast(FP8X4),
+                    rhs_scale=planes[h, z][:],
+                    start=(z == 0),
+                    stop=(z == PASSES - 1),
+                )
+            if h == 0:
+                for i in range(BLOCKS):
+                    nc.scalar.activation(squares[:, BLOCKS + i, cols], a_sums[i][:, cols], ACT.Square, scale=inv_b[:, i : i + 1], accum_out=ssq_a[h][:, i : i + 1])
+                b_part = [sb.tile([P, N], F32, name="b_part%d" % i, tag="staging%d" % (0, 3, 2, 1)[i], align_bytes=64) for i in range(BLOCKS)]
+                for i in range(BLOCKS):
+                    if i in ():
+                        nc.scalar.activation(b_part[i][:], b_sums[i][:], ACT.Copy, scale=0.3)
+                    else:
+                        nc.vector.tensor_scalar(b_part[i][:], b_sums[i][:], 0.3, None, MULT)
+
+        partial = sb.tile([P, BLOCKS], F32, name="partial")
+        for pair in range(2):
+            two = slice(2 * pair, 2 * pair + 2)
+            nc.gpsimd.tensor_tensor(partial[:, two], ssq_a[0][:, two], eps_a[:, two], ADD)
+        ratio = sb.tile([P, BLOCKS], F32, name="ratio")
+        for i in range(BLOCKS):
+            nc.scalar.activation(squares[:, BLOCKS + i, HALF:], a_sums[i][:, HALF:], ACT.Square, scale=inv_b[:, i : i + 1], accum_out=ssq_a[1][:, i : i + 1])
+            nc.scalar.activation(ratio[:, i : i + 1], ssq_a[1][:, i : i + 1], ACT.Abs_reciprocal_sqrt, bias=partial[:, i : i + 1])
+            result = sb.tile([P, N], F32, name="result%d" % i)
+            nc.vector.scalar_tensor_tensor(result[:], a_sums[i][:], ratio[:, i : i + 1], b_part[i][:], MULT, ADD)
+            nc.sync.dma_start(out[i * P : (i + 1) * P, :], result[:])

@@ -28,12 +28,13 @@ def tile_moe_expert_sized_like_other_kernel(tc, xt_words, xt_scales, wa, wb_word
     nc = tc.nc
     with ExitStack() as ctx:
         sb = ctx.enter_context(tc.tile_pool(name="sb", bufs=1))
+        shared = ctx.enter_context(tc.tile_pool(name="shared", bufs=1))
         psum = ctx.enter_context(tc.psum_pool(name="psum", bufs=1))
 
         list_a = sb.tile([P, J // 16], U16, name="list_a")
         list_b = sb.tile([P, J // 16], U16, name="list_b")
         x_words = [sb.tile([P, T], I32, name="x_words%d" % z, align_bytes=64) for z in range(PASSES)]
-        x_scales = sb.tile([P, T], U8, name="x_scales", align_bytes=64)
+        x_scales = shared.tile([P, T], U8, name="x_scales", offset=7168)
         wb_codes = sb.tile([P, PASSES, 2 * N], U8, name="wb_codes", align_bytes=64)
         wb_plane = sb.tile([P, PASSES, N], U8, name="wb_plane", align_bytes=64)
         xb_plane1 = sb.tile([P, J], U8, name="xb_plane1", align_bytes=64)
@@ -53,11 +54,6 @@ def tile_moe_expert_sized_like_other_kernel(tc, xt_words, xt_scales, wa, wb_word
         for r in range(4):
             nc.sync.dma_start(wb_plane[r:P:32, :, :].bitcast(I32), wb_scales.rearrange("z (q r) c -> r q z c", r=4)[r].bitcast(I32))
         nc.sync.dma_start(x_words[1][:], xt_words[1].rearrange("p c t -> p (c t)").bitcast(I32))
-        wa_raw = {}
-        for h in range(2):
-            for z in range(PASSES):
-                wa_raw[h, z] = sb.tile([P, 4, HALF], F32, name="wa_raw%d_%d" % (h, z))
-                nc.sync.dma_start(wa_raw[h, z][:], wa[512 * z : 512 * (z + 1), h * HALF : (h + 1) * HALF].rearrange("(p t) c -> p t c", t=4))
 
         root_eps = sb.tile([P, 1], F32, name="root_eps")
         nc.scalar.activation(root_eps[:], zero[:], ACT.Abs_reciprocal_sqrt, bias=1.0 / EPS_SUM)
@@ -69,6 +65,9 @@ def tile_moe_expert_sized_like_other_kernel(tc, xt_words, xt_scales, wa, wb_word
         nc.vector.tensor_copy(xb_plane[:], x_scales[:].indirect(list_b[:]))
         nc.scalar.dma_start(xb_plane1[0:100, :].bitcast(I32), xb_plane[4:104, :].bitcast(I32))
         nc.vector.tensor_copy(xa_plane[:], x_scales[:].indirect(list_a[:]))
+        wa_raw = [shared.tile([P, 4, N], F32, name="wa_raw%d" % z, offset=8192 * z) for z in range(PASSES)]
+        for z in range(PASSES):
+            nc.sync.dma_start(wa_raw[z][:], wa[512 * z : 512 * (z + 1), :].rearrange("(p t) c -> p t c", t=4))
         nc.vector.tensor_copy(xb[0][:], x_words[0][:].bitcast(U32).indirect(list_b[:]))
         nc.vector.tensor_copy(xa[0][:], x_words[0][:].bitcast(U32).indirect(list_a[:]))
         for h in range(2):
@@ -91,68 +90,59 @@ def tile_moe_expert_sized_like_other_kernel(tc, xt_words, xt_scales, wa, wb_word
                     stop=(z == PASSES - 1),
                 )
 
+        a_sums = [psum.tile([P, N], F32, name="a_sums%d" % i) for i in range(BLOCKS)]
+
         ssq_b = sb.tile([P, BLOCKS], F32, name="ssq_b")
         inv_b = sb.tile([P, BLOCKS], F32, name="inv_b")
         eps_a = sb.tile([P, BLOCKS], F32, name="eps_a")
-        squares = sb.tile([P, 2 * BLOCKS, N], BF16, name="squares")
+        squares = sb.tile([P, BLOCKS, N], BF16, name="squares")
+        staged = [sb.tile([P, N, 4], BF16, name="grouped%d" % z, align_bytes=64) for z in range(PASSES)]
+        spare = staged[1][:].rearrange("p c t -> p (c t)")
         for i in range(BLOCKS):
-            nc.scalar.activation(squares[:, i, :], b_sums[i][:], ACT.Square, accum_out=ssq_b[:, i : i + 1])
+            nc.scalar.activation(spare[:, i * N : (i + 1) * N], b_sums[i][:], ACT.Square, accum_out=ssq_b[:, i : i + 1])
         nc.scalar.activation(inv_b[:], ssq_b[:], ACT.Abs_reciprocal_sqrt, bias=EPS_SUM)
         nc.scalar.activation(eps_a[:], inv_b[:], ACT.Square, scale=root_eps[:])
 
-        codes, planes = {}, {}
-        for h in range(2):
-            for z in range(PASSES):
-                grouped = sb.tile([P, HALF, 4], BF16, name="grouped%d_%d" % (h, z), tag="staging%d" % (0, 1, 2, 1)[2 * h + z], align_bytes=64)
-                codes[h, z] = sb.tile([P, HALF], U32, name="codes%d_%d" % (h, z), align_bytes=64)
-                planes[h, z] = sb.tile([P, HALF], U8, name="plane%d_%d" % (h, z), align_bytes=64)
-                if (h, z) in ((0, 0), (0, 1), (1, 0)):
-                    nc.gpsimd.tensor_scalar(grouped[:], wa_raw[h, z][:].rearrange("p t c -> p c t"), 1.0, 0.0, MULT, ADD)
-                elif (h, z) in ():
-                    nc.scalar.copy(
-                        grouped[:].rearrange("p (c i) t -> p c t i", i=4),
-                        wa_raw[h, z][:].rearrange("p t (c i) -> p c t i", i=4),
-                    )
-                else:
-                    nc.vector.tensor_copy(
-                        grouped[:].rearrange("p (c i) t -> p c t i", i=4),
-                        wa_raw[h, z][:].rearrange("p t (c i) -> p c t i", i=4),
-                    )
-                nc.vector.quantize_mx(out=codes[h, z][:].bitcast(FP8X4), scales=planes[h, z][:], in_=grouped[:].rearrange("p c t -> p (c t)"))
-
-        a_sums = [psum.tile([P, N], F32, name="a_sums%d" % i) for i in range(BLOCKS)]
-        ssq_a = [sb.tile([P, BLOCKS], F32, name="ssq_a%d" % h) for h in range(2)]
-        for h in range(2):
-            cols = slice(h * HALF, (h + 1) * HALF)
-            for z, i in [(z, i) for z in range(PASSES) for i in range(BLOCKS)]:
+        for z in range(PASSES):
+            grouped = staged[z]
+            codes = sb.tile([P, N], U32, name="codes%d" % z, align_bytes=64)
+            plane = sb.tile([P, N], U8, name="plane%d" % z, align_bytes=64)
+            cut = (512, 320)[z]
+            for lo, hi in ((0, HALF), (HALF, cut)):
+                nc.vector.tensor_copy(
+                    grouped[:, lo:hi, :].rearrange("p (c i) t -> p c t i", i=4),
+                    wa_raw[z][:, :, lo:hi].rearrange("p t (c i) -> p c t i", i=4),
+                )
+            if cut < N:
+                nc.scalar.copy(grouped[:, cut:, :], wa_raw[z][:, :, cut:].rearrange("p t c -> p c t"))
+            for lo, hi in ((0, HALF), (HALF, N)):
+                nc.vector.quantize_mx(out=codes[:, lo:hi].bitcast(FP8X4), scales=plane[:, lo:hi], in_=grouped[:, lo:hi, :].rearrange("p c t -> p (c t)"))
+            for i in range(BLOCKS):
                 slots = slice(i * P, (i + 1) * P)
                 nc.tensor.matmul_mx(
-                    out=a_sums[i][:, cols],
+                    out=a_sums[i][:],
                     lhsT=xa[z][:, slots].bitcast(FP8X4),
                     lhsT_scale=xa_plane[4 * z :, slots],
-                    rhs=codes[h, z][:].bitcast(FP8X4),
-                    rhs_scale=planes[h, z][:],
+                    rhs=codes[:].bitcast(FP8X4),
+                    rhs_scale=plane[:],
                     start=(z == 0),
                     stop=(z == PASSES - 1),
                 )
-            if h == 0:
-                for i in range(BLOCKS):
-                    nc.scalar.activation(squares[:, BLOCKS + i, cols], a_sums[i][:, cols], ACT.Square, scale=inv_b[:, i : i + 1], accum_out=ssq_a[h][:, i : i + 1])
-                b_part = [sb.tile([P, N], F32, name="b_part%d" % i, tag="staging%d" % (0, 3, 2, 1)[i], align_bytes=64) for i in range(BLOCKS)]
-                for i in range(BLOCKS):
-                    if i in ():
-                        nc.scalar.activation(b_part[i][:], b_sums[i][:], ACT.Copy, scale=0.3)
-                    else:
-                        nc.vector.tensor_scalar(b_part[i][:], b_sums[i][:], 0.3, None, MULT)
 
-        partial = sb.tile([P, BLOCKS], F32, name="partial")
-        for pair in range(2):
-            two = slice(2 * pair, 2 * pair + 2)
-            nc.gpsimd.tensor_tensor(partial[:, two], ssq_a[0][:, two], eps_a[:, two], ADD)
+        b_low = shared.tile([P, 2, N], F32, name="b_low", offset=8192)
+        b_high = sb.tile([P, 2, N], F32, name="b_high", tag="grouped1", align_bytes=64)
+        b_part = [b_low[:, 0, :], b_low[:, 1, :], b_high[:, 0, :], b_high[:, 1, :]]
+        for i in range(BLOCKS):
+            if i < 2:
+                nc.scalar.activation(b_part[i], b_sums[i][:], ACT.Copy, scale=0.3)
+            else:
+                nc.vector.tensor_scalar(b_part[i], b_sums[i][:], 0.3, None, MULT)
+
+        ssq_a = sb.tile([P, BLOCKS], F32, name="ssq_a")
         ratio = sb.tile([P, BLOCKS], F32, name="ratio")
         for i in range(BLOCKS):
-            nc.scalar.activation(squares[:, BLOCKS + i, HALF:], a_sums[i][:, HALF:], ACT.Square, scale=inv_b[:, i : i + 1], accum_out=ssq_a[1][:, i : i + 1])
-            nc.scalar.activation(ratio[:, i : i + 1], ssq_a[1][:, i : i + 1], ACT.Abs_reciprocal_sqrt, bias=partial[:, i : i + 1])
+            nc.scalar.activation(squares[:, i, :], a_sums[i][:], ACT.Square, scale=inv_b[:, i : i + 1], accum_out=ssq_a[:, i : i + 1])
+            nc.scalar.activation(ratio[:, i : i + 1], ssq_a[:, i : i + 1], ACT.Abs_reciprocal_sqrt, bias=eps_a[:, i : i + 1])
             result = sb.tile([P, N], F32, name="result%d" % i)
-            nc.vector.scalar_tensor_tensor(result[:], a_sums[i][:], ratio[:, i : i + 1], b_part[i][:], MULT, ADD)
+            nc.vector.scalar_tensor_tensor(result[:], a_sums[i][:], ratio[:, i : i + 1], b_part[i], MULT, ADD)
             nc.sync.dma_start(out[i * P : (i + 1) * P, :], result[:])

@@ -68,7 +68,8 @@ def tile_moe_expert_sized_like_other_kernel(tc, xt_words, xt_scales, wa, wb_word
         wa_raw = [shared.tile([P, 4, N], F32, name="wa_raw%d" % z, offset=8192 * z) for z in range(PASSES)]
         for z in range(PASSES):
             nc.sync.dma_start(wa_raw[z][:], wa[512 * z : 512 * (z + 1), :].rearrange("(p t) c -> p t c", t=4))
-        nc.vector.tensor_copy(xb[0][:], x_words[0][:].bitcast(U32).indirect(list_b[:]))
+        for h in range(2):
+            nc.vector.tensor_copy(xb[0][:, h * 256 : (h + 1) * 256], x_words[0][:].bitcast(U32).indirect(list_b[:, h * 16 : (h + 1) * 16]))
         nc.vector.tensor_copy(xa[0][:], x_words[0][:].bitcast(U32).indirect(list_a[:]))
         for h in range(2):
             nc.vector.tensor_copy(xb[1][:, h * 256 : (h + 1) * 256], x_words[1][:].bitcast(U32).indirect(list_b[:, h * 16 : (h + 1) * 16]))
@@ -96,12 +97,10 @@ def tile_moe_expert_sized_like_other_kernel(tc, xt_words, xt_scales, wa, wb_word
         inv_b = sb.tile([P, BLOCKS], F32, name="inv_b")
         eps_a = sb.tile([P, BLOCKS], F32, name="eps_a")
         squares = sb.tile([P, BLOCKS, N], BF16, name="squares")
-        staged = [sb.tile([P, N, 4], BF16, name="grouped%d" % z, align_bytes=64) for z in range(PASSES)]
-        spare = staged[1][:].rearrange("p c t -> p (c t)")
+        staged = [sb.tile([P, 4 * N], BF16, name="grouped%d" % z, align_bytes=64) for z in range(PASSES)]
+        spare = staged[1]
         for i in range(BLOCKS):
             nc.scalar.activation(spare[:, i * N : (i + 1) * N], b_sums[i][:], ACT.Square, accum_out=ssq_b[:, i : i + 1])
-        nc.scalar.activation(inv_b[:], ssq_b[:], ACT.Abs_reciprocal_sqrt, bias=EPS_SUM)
-        nc.scalar.activation(eps_a[:], inv_b[:], ACT.Square, scale=root_eps[:])
 
         for z in range(PASSES):
             grouped = staged[z]
@@ -110,13 +109,13 @@ def tile_moe_expert_sized_like_other_kernel(tc, xt_words, xt_scales, wa, wb_word
             cut = (512, 320)[z]
             for lo, hi in ((0, HALF), (HALF, cut)):
                 nc.vector.tensor_copy(
-                    grouped[:, lo:hi, :].rearrange("p (c i) t -> p c t i", i=4),
+                    grouped[:, 4 * lo : 4 * hi].rearrange("p (c i t) -> p c t i", i=4, t=4),
                     wa_raw[z][:, :, lo:hi].rearrange("p t (c i) -> p c t i", i=4),
                 )
             if cut < N:
-                nc.scalar.copy(grouped[:, cut:, :], wa_raw[z][:, :, cut:].rearrange("p t c -> p c t"))
+                nc.scalar.copy(grouped[:, 4 * cut :].rearrange("p (c t) -> p c t", t=4), wa_raw[z][:, :, cut:].rearrange("p t c -> p c t"))
             for lo, hi in ((0, HALF), (HALF, N)):
-                nc.vector.quantize_mx(out=codes[:, lo:hi].bitcast(FP8X4), scales=plane[:, lo:hi], in_=grouped[:, lo:hi, :].rearrange("p c t -> p (c t)"))
+                nc.vector.quantize_mx(out=codes[:, lo:hi].bitcast(FP8X4), scales=plane[:, lo:hi], in_=grouped[:, 4 * lo : 4 * hi])
             for i in range(BLOCKS):
                 slots = slice(i * P, (i + 1) * P)
                 nc.tensor.matmul_mx(
@@ -129,11 +128,13 @@ def tile_moe_expert_sized_like_other_kernel(tc, xt_words, xt_scales, wa, wb_word
                     stop=(z == PASSES - 1),
                 )
 
-        b_low = shared.tile([P, 2, N], F32, name="b_low", offset=8192)
-        b_high = sb.tile([P, 2, N], F32, name="b_high", tag="grouped1", align_bytes=64)
-        b_part = [b_low[:, 0, :], b_low[:, 1, :], b_high[:, 0, :], b_high[:, 1, :]]
+        nc.scalar.activation(inv_b[:], ssq_b[:], ACT.Abs_reciprocal_sqrt, bias=EPS_SUM)
+        nc.scalar.activation(eps_a[:], inv_b[:], ACT.Square, scale=root_eps[:])
+        b_low = shared.tile([P, 1, N], F32, name="b_low", offset=8192)
+        b_high = sb.tile([P, 3, N], F32, name="b_high", tag="grouped1", align_bytes=64)
+        b_part = [b_low[:, 0, :], b_high[:, 0, :], b_high[:, 1, :], b_high[:, 2, :]]
         for i in range(BLOCKS):
-            if i < 2:
+            if i < 1:
                 nc.scalar.activation(b_part[i], b_sums[i][:], ACT.Copy, scale=0.3)
             else:
                 nc.vector.tensor_scalar(b_part[i], b_sums[i][:], 0.3, None, MULT)

@@ -92,7 +92,16 @@ def tile_moe_expert_sized_like_other_kernel(tc, xt_words, xt_scales, wa, wb_word
                 )
 
         a_sums = [psum.tile([P, N], F32, name="a_sums%d" % i) for i in range(BLOCKS)]
-
+        for i in range(2):
+            nc.tensor.matmul_mx(
+                out=a_sums[i][:],
+                lhsT=xa[1][:, :P].bitcast(FP8X4),
+                lhsT_scale=xb_plane[:, :P],
+                rhs=wb_codes[:, 0, :].bitcast(FP4X4),
+                rhs_scale=wb_plane[:, 0, :],
+                start=True,
+                stop=True,
+            )
         ssq_b = sb.tile([P, BLOCKS], F32, name="ssq_b")
         inv_b = sb.tile([P, BLOCKS], F32, name="inv_b")
         eps_a = sb.tile([P, BLOCKS], F32, name="eps_a")
@@ -106,7 +115,7 @@ def tile_moe_expert_sized_like_other_kernel(tc, xt_words, xt_scales, wa, wb_word
             grouped = staged[z]
             codes = sb.tile([P, N], U32, name="codes%d" % z, align_bytes=64)
             plane = sb.tile([P, N], U8, name="plane%d" % z, align_bytes=64)
-            cut = (512, 320)[z]
+            cut = (512, 384)[z]
             for lo, hi in ((0, HALF), (HALF, cut)):
                 nc.vector.tensor_copy(
                     grouped[:, 4 * lo : 4 * hi].rearrange("p (c i t) -> p c t i", i=4, t=4),

from contextlib import ExitStack

import concourse.mybir as mybir

K, T, J, N = 1024, 2048, 512, 512
FLOPS = 2 * 2 * J * N * K

F32 = mybir.dt.float32
BF16 = mybir.dt.bfloat16
I32 = mybir.dt.int32
U32 = mybir.dt.uint32
U16 = mybir.dt.uint16
U8 = mybir.dt.uint8
FP8X4 = mybir.dt.float8_e4m3fn_x4
FP4X4 = mybir.dt.float4_e2m1fn_x4
ACT = mybir.ActivationFunctionType
MULT = mybir.AluOpType.mult
ADD = mybir.AluOpType.add

P = 128
PASSES = 2
BLOCKS = J // P
HALF = N // 2
EPS_SUM = 0.01 * N


def tile_moe_expert_sized_like_other_kernel(tc, xt_words, xt_scales, wa, wb_words, wb_scales, offs, offs2, out):
    nc = tc.nc
    with ExitStack() as ctx:
        sb = ctx.enter_context(tc.tile_pool(name="sb", bufs=1))
        shared = ctx.enter_context(tc.tile_pool(name="shared", bufs=1))
        psum = ctx.enter_context(tc.psum_pool(name="psum", bufs=1))

        list_a = sb.tile([P, J // 16], U16, name="list_a")
        list_b = sb.tile([P, J // 16], U16, name="list_b")
        x_words = [sb.tile([P, T], I32, name="x_words%d" % z, align_bytes=64) for z in range(PASSES)]
        x_scales = shared.tile([P, T], U8, name="x_scales", offset=7168)
        wb_codes = sb.tile([P, PASSES, 2 * N], U8, name="wb_codes", align_bytes=64)
        wb_plane = sb.tile([P, PASSES, N], U8, name="wb_plane", align_bytes=64)
        xb_plane1 = sb.tile([P, J], U8, name="xb_plane1", align_bytes=64)
        zero = sb.tile([P, 1], F32, name="zero")

        nc.vector.memset(x_scales[:].bitcast(I32), 0)
        nc.vector.memset(wb_plane[:].rearrange("p z c -> p (z c)").bitcast(I32), 0)
        nc.vector.memset(xb_plane1[:].bitcast(I32), 0)
        nc.vector.memset(zero[:], 0.0)

        nc.sync.dma_start(list_b[:], offs2)
        nc.sync.dma_start(list_a[:], offs)
        nc.sync.dma_start(wb_codes[:].bitcast(I32), wb_words.rearrange("z p c -> p z c").bitcast(I32))
        for q in range(4):
            nc.sync.dma_start(x_scales[32 * q : 32 * q + 8, :].bitcast(I32), xt_scales[:, 4 * q : 4 * q + 4, :].bitcast(I32))
        nc.sync.dma_start(x_words[0][:], xt_words[0].rearrange("p c t -> p (c t)").bitcast(I32))
        for r in range(4):
            nc.sync.dma_start(wb_plane[r:P:32, :, :].bitcast(I32), wb_scales.rearrange("z (q r) c -> r q z c", r=4)[r].bitcast(I32))
        nc.sync.dma_start(x_words[1][:], xt_words[1].rearrange("p c t -> p (c t)").bitcast(I32))

        root_eps = sb.tile([P, 1], F32, name="root_eps")
        nc.scalar.activation(root_eps[:], zero[:], ACT.Abs_reciprocal_sqrt, bias=1.0 / EPS_SUM)

        xa_plane = sb.tile([P, J], U8, name="xa_plane", align_bytes=64)
        xb_plane = sb.tile([P, J], U8, name="xb_plane", align_bytes=64)
        xa = [sb.tile([P, J], U32, name="xa%d" % z, align_bytes=64) for z in range(PASSES)]
        xb = [sb.tile([P, J], U32, name="xb%d" % z, align_bytes=64) for z in range(PASSES)]
        nc.vector.tensor_copy(xb_plane[:], x_scales[:].indirect(list_b[:]))
        nc.scalar.dma_start(xb_plane1[0:100, :].bitcast(I32), xb_plane[4:104, :].bitcast(I32))
        nc.vector.tensor_copy(xa_plane[:], x_scales[:].indirect(list_a[:]))
        wa_raw = [shared.tile([P, 4, N], F32, name="wa_raw%d" % z, offset=8192 * z) for z in range(PASSES)]
        for z in range(PASSES):
            nc.sync.dma_start(wa_raw[z][:], wa[512 * z : 512 * (z + 1), :].rearrange("(p t) c -> p t c", t=4))
        for h in range(2):
            nc.vector.tensor_copy(xb[0][:, h * 256 : (h + 1) * 256], x_words[0][:].bitcast(U32).indirect(list_b[:, h * 16 : (h + 1) * 16]))
        nc.vector.tensor_copy(xa[0][:], x_words[0][:].bitcast(U32).indirect(list_a[:]))
        for h in range(2):
            nc.vector.tensor_copy(xb[1][:, h * 256 : (h + 1) * 256], x_words[1][:].bitcast(U32).indirect(list_b[:, h * 16 : (h + 1) * 16]))
        nc.vector.tensor_copy(xa[1][:], x_words[1][:].bitcast(U32).indirect(list_a[:]))


        b_sums = [psum.tile([P, N], F32, name="b_sums%d" % i, tag="bank_b%d" % i) for i in range(BLOCKS)]
        xb_planes = [xb_plane, xb_plane1]
        for z in range(PASSES):
            for i in range(BLOCKS):
                slots = slice(i * P, (i + 1) * P)
                nc.tensor.matmul_mx(
                    out=b_sums[i][:],
                    lhsT=xb[z][:, slots].bitcast(FP8X4),
                    lhsT_scale=xb_planes[z][:, slots],
                    rhs=wb_codes[:, z, :].bitcast(FP4X4),
                    rhs_scale=wb_plane[:, z, :],
                    start=(z == 0),
                    stop=(z == PASSES - 1),
                )

        a_sums = [psum.tile([P, N], F32, name="a_sums%d" % i) for i in range(BLOCKS)]
        for i in range(2):
            nc.tensor.matmul_mx(
                out=a_sums[i][:],
                lhsT=xa[1][:, :P].bitcast(FP8X4),
                lhsT_scale=xb_plane[:, :P],
                rhs=wb_codes[:, 0, :].bitcast(FP4X4),
                rhs_scale=wb_plane[:, 0, :],
                start=True,
                stop=True,
            )
        ssq_b = sb.tile([P, BLOCKS], F32, name="ssq_b")
        inv_b = sb.tile([P, BLOCKS], F32, name="inv_b")
        eps_a = sb.tile([P, BLOCKS], F32, name="eps_a")
        squares = sb.tile([P, BLOCKS, N], BF16, name="squares")
        staged = [sb.tile([P, 4 * N], BF16, name="grouped%d" % z, align_bytes=64) for z in range(PASSES)]
        spare = staged[1]
        for i in range(BLOCKS):
            nc.scalar.activation(spare[:, i * N : (i + 1) * N], b_sums[i][:], ACT.Square, accum_out=ssq_b[:, i : i + 1])

        for z in range(PASSES):
            grouped = staged[z]
            codes = sb.tile([P, N], U32, name="codes%d" % z, align_bytes=64)
            plane = sb.tile([P, N], U8, name="plane%d" % z, align_bytes=64)
            cut = (512, 384)[z]
            for lo, hi in ((0, HALF), (HALF, cut)):
                nc.vector.tensor_copy(
                    grouped[:, 4 * lo : 4 * hi].rearrange("p (c i t) -> p c t i", i=4, t=4),
                    wa_raw[z][:, :, lo:hi].rearrange("p t (c i) -> p c t i", i=4),
                )
            if cut < N:
                nc.scalar.copy(grouped[:, 4 * cut :].rearrange("p (c t) -> p c t", t=4), wa_raw[z][:, :, cut:].rearrange("p t c -> p c t"))
            for lo, hi in ((0, HALF), (HALF, N)):
                nc.vector.quantize_mx(out=codes[:, lo:hi].bitcast(FP8X4), scales=plane[:, lo:hi], in_=grouped[:, 4 * lo : 4 * hi])
            for i in range(BLOCKS):
                slots = slice(i * P, (i + 1) * P)
                nc.tensor.matmul_mx(
                    out=a_sums[i][:],
                    lhsT=xa[z][:, slots].bitcast(FP8X4),
                    lhsT_scale=xa_plane[4 * z :, slots],
                    rhs=codes[:].bitcast(FP8X4),
                    rhs_scale=plane[:],
                    start=(z == 0),
                    stop=(z == PASSES - 1),
                )

        nc.scalar.activation(inv_b[:], ssq_b[:], ACT.Abs_reciprocal_sqrt, bias=EPS_SUM)
        nc.scalar.activation(eps_a[:], inv_b[:], ACT.Square, scale=root_eps[:])
        b_low = shared.tile([P, 1, N], F32, name="b_low", offset=8192)
        b_high = sb.tile([P, 3, N], F32, name="b_high", tag="grouped1", align_bytes=64)
        b_part = [b_low[:, 0, :], b_high[:, 0, :], b_high[:, 1, :], b_high[:, 2, :]]
        for i in range(BLOCKS):
            if i < 1:
                nc.scalar.activation(b_part[i], b_sums[i][:], ACT.Copy, scale=0.3)
            else:
                nc.vector.tensor_scalar(b_part[i], b_sums[i][:], 0.3, None, MULT)

        ssq_a = sb.tile([P, BLOCKS], F32, name="ssq_a")
        ratio = sb.tile([P, BLOCKS], F32, name="ratio")
        for i in range(BLOCKS):
            nc.scalar.activation(squares[:, i, :], a_sums[i][:], ACT.Square, scale=inv_b[:, i : i + 1], accum_out=ssq_a[:, i : i + 1])
            nc.scalar.activation(ratio[:, i : i + 1], ssq_a[:, i : i + 1], ACT.Abs_reciprocal_sqrt, bias=eps_a[:, i : i + 1])
            result = sb.tile([P, N], F32, name="result%d" % i)
            nc.vector.scalar_tensor_tensor(result[:], a_sums[i][:], ratio[:, i : i + 1], b_part[i], MULT, ADD)
            nc.sync.dma_start(out[i * P : (i + 1) * P, :], result[:])
